import numpy as np
import ml_dtypes


def mxq(x, axis, fmt="e4m3"):
    dtype, down = {"e4m3": (ml_dtypes.float8_e4m3fn, 7), "e5m2": (ml_dtypes.float8_e5m2, 14)}[fmt]
    v = np.moveaxis(np.asarray(x, np.float32).astype(ml_dtypes.bfloat16).astype(np.float64), axis, -1)
    blocks = v.reshape(v.shape[:-1] + (-1, 32))
    amax = np.abs(blocks).max(-1, keepdims=True)
    byte = np.maximum(np.where(amax > 0, np.frexp(amax)[1] - 1 + 127, 0) - down, 1)
    scale = np.exp2(byte - 127.0)
    codes = (blocks / scale).astype(np.float32).astype(dtype).astype(np.float64)
    return np.moveaxis((codes * scale).reshape(v.shape), -1, axis)


WIDE = False


def mx_kscale(k):
    if not WIDE:
        return np.ones(k)
    levels = np.array([10, -10, 5, -5, 0])
    if k % 512:
        return np.exp2(np.random.permutation(np.resize(levels, k // 32))).repeat(32)
    a = np.empty((k // 512, 16))
    for p in range(k // 512):
        a[p, :8] = np.random.permutation(np.resize(levels, 8))
        for g in range(8):
            far = levels[np.abs(levels - a[p, g]) >= 10]
            a[p, g + 8] = far[np.random.randint(len(far))]
    return np.exp2(a.ravel()).repeat(32)


def f64(x):
    return np.asarray(x).astype(np.float64)


def striped(idx):
    return np.tile(idx.reshape(-1, 16).T, (8, 1)).astype(np.uint16)


def unstriped(offs):
    return offs[:16].T.reshape(-1).astype(np.int64)


def gelu(v):
    return 0.5 * v * (1.0 + np.tanh(np.sqrt(2.0 / np.pi) * (v + 0.044715 * v**3)))


K, T, E, C, H, N = 512, 512, 8, 128, 512, 128


def by_expert(wq, xq):
    return np.concatenate([wq[e].T @ xq[:, e * C:(e + 1) * C] for e in range(E)], axis=1)


def setup_inputs():
    n = np.random.standard_normal
    s = mx_kscale(K)[:, None]
    u = mx_kscale(H)
    first = np.random.permutation(np.repeat(np.arange(E), T // E))
    second = (first + 1 + np.random.permutation(np.repeat(np.arange(E - 1), -(-T // (E - 1)))[:T])) % E
    while np.bincount(second, minlength=E).max() != T // E:
        load = np.bincount(second, minlength=E); hi, lo = int(load.argmax()), int(load.argmin())
        t = np.flatnonzero((second == hi) & (first != lo))[0]; second[t] = lo
    slot_token = np.empty(E * C, np.int64); pos = np.empty((2, T), np.int64); fill = np.zeros(E, np.int64)
    place = np.stack([np.random.permutation(C) for _ in range(E)])
    for r, deal in enumerate((first, second)):
        for t in np.random.permutation(T):
            e = deal[t]; j = e * C + place[e, fill[e]]; fill[e] += 1; slot_token[j] = t; pos[r, t] = j
    g = np.random.uniform(0.2, 0.8, T)
    return {
        "xT": (n((K, T)) * s).astype(np.float32),
        "w1": (n((E, K, H)) / np.sqrt(K) / s[None] * u[None, None, :]).astype(np.float32),
        "w2": (n((E, H, N)) / np.sqrt(H) / u[None, :, None]).astype(np.float32),
        "gate": np.stack([np.tile(g, (N, 1)), np.tile(1.0 - g, (N, 1))]).astype(np.float32),
        "offs": striped(slot_token),
        "pos1": striped(pos[0]),
        "pos2": striped(pos[1]),
    }


def reference(xT, w1, w2, gate, offs, pos1, pos2):
    idx = unstriped(offs)
    xq = mxq(f64(xT)[:, idx], 0, "e4m3")
    h = gelu(by_expert(mxq(f64(w1), 1, "e4m3"), xq))
    y = by_expert(mxq(f64(w2), 1, "e4m3"), mxq(h, 0, "e4m3"))
    return f64(gate[0]) * y[:, unstriped(pos1)] + f64(gate[1]) * y[:, unstriped(pos2)]

@@ -1,0 +1,212 @@
+from contextlib import ExitStack
+
+import concourse.mybir as mybir
+
+K, T, E, C, H, N = 512, 512, 8, 128, 512, 128
+FLOPS = 2 * E * C * (K * H + H * N)
+
+F32 = mybir.dt.float32
+BF16 = mybir.dt.bfloat16
+U32 = mybir.dt.uint32
+U16 = mybir.dt.uint16
+U8 = mybir.dt.uint8
+FP8X4 = mybir.dt.float8_e4m3fn_x4
+ACT = mybir.ActivationFunctionType
+ALU = mybir.AluOpType
+
+P = 128
+PACK = 4
+
+MV = (0, 48, 16, 80, 80, 80, 96, 128)
+XH = 256
+GCUT = 256
+H_AFTER_W2 = {7: 4}
+H_IN_W2_RAW = {5: 0, 7: 2}
+W2_BEFORE_H = {5: 0, 6: 1, 7: 2}
+S_W2 = (0, 2)
+W2_CUT = (0, 2, 4, 6, 7, 8)
+Y_CUT = (0, 4, 6, 7, 8)
+LAG = 2
+
+
+def tile_routed_moe_kernel(tc, xT, w1, w2, gate, offs, pos1, pos2, out):
+    nc = tc.nc
+    with ExitStack() as ctx:
+        lists = ctx.enter_context(tc.tile_pool(name="lists", bufs=1))
+        keep = ctx.enter_context(tc.tile_pool(name="keep", bufs=1))
+        ring = ctx.enter_context(tc.tile_pool(name="ring", bufs=E - LAG))
+        psum_a = ctx.enter_context(tc.psum_pool(name="psum_a", bufs=4))
+        psum_y = ctx.enter_context(tc.psum_pool(name="psum_y", bufs=1))
+
+        offs_t = lists.tile([P, E * C // 16], U16, name="offs_t")
+        nc.sync.dma_start(offs_t[:], offs)
+        x_view = xT.rearrange("(p j) t -> p j t", j=PACK)
+        x_raw = []
+        for u in range(T // XH):
+            raw = keep.tile([P, PACK, XH], F32, name="x_raw%d" % u)
+            nc.sync.dma_start(raw[:], x_view[:, :, u * XH : (u + 1) * XH])
+            x_raw.append(raw)
+        w1_raw = []
+        for e in range(E):
+            if e < LAG:
+                raw = keep.tile([P, PACK, H], F32, name="w1_raw%d" % e)
+            else:
+                raw = ring.tile([P, PACK, H], F32, name="w1_raw%d" % e, tag="ring", align_bytes=64)
+            nc.sync.dma_start(raw[:], w1[e, :, :].rearrange("(p j) c -> p j c", j=PACK))
+            w1_raw.append(raw)
+        pos1_t = lists.tile([P, T // 16], U16, name="pos1_t")
+        nc.sync.dma_start(pos1_t[:], pos1)
+        pos2_t = lists.tile([P, T // 16], U16, name="pos2_t")
+        nc.sync.dma_start(pos2_t[:], pos2)
+        w2_raw = []
+        for q in range(len(W2_CUT) - 1):
+            raw = keep.tile(
+                [P, W2_CUT[q + 1] - W2_CUT[q], PACK * N], F32, name="w2_raw%d" % q, tag="w2_raw%d" % q, align_bytes=64
+            )
+            nc.sync.dma_start(
+                raw[:], w2[W2_CUT[q] : W2_CUT[q + 1], :, :].rearrange("e (p j) n -> p e (j n)", j=PACK)
+            )
+            w2_raw.append(raw)
+        gate_t = keep.tile([P, 2, T], F32, name="gate_t")
+        nc.sync.dma_start(gate_t[:], gate.rearrange("r n t -> n r t"))
+
+        warm_in = keep.tile([P, 1], F32, name="warm_in")
+        warm_out = keep.tile([P, 1], F32, name="warm_out")
+        nc.vector.memset(warm_in[:], 0.0)
+        nc.scalar.activation(warm_out[:], warm_in[:], ACT.Gelu_apprx_tanh)
+        x_scales = keep.tile([P, T], U8, name="x_scales", align_bytes=64)
+        nc.gpsimd.memset(x_scales[:], 0)
+
+        x_grp = keep.tile([P, T, PACK], BF16, name="x_grp", align_bytes=64)
+        for u in range(T // XH):
+            nc.vector.tensor_copy(
+                x_grp[:, u * XH : (u + 1) * XH, :].rearrange("p (c i) j -> p c j i", i=4),
+                x_raw[u][:].rearrange("p j (c i) -> p c j i", i=4),
+            )
+        x_codes = keep.tile([P, T], U32, name="x_codes", align_bytes=64)
+        nc.vector.quantize_mx(
+            out=x_codes[:].bitcast(FP8X4), scales=x_scales[:], in_=x_grp[:].rearrange("p t j -> p (t j)")
+        )
+        g_codes = []
+        g_scales = []
+
+        def gather(c):
+            cols = slice(c * GCUT // 16, (c + 1) * GCUT // 16)
+            gc = keep.tile([P, GCUT], U32, name="g_codes%d" % c, align_bytes=64)
+            nc.vector.tensor_copy(gc[:], x_codes[:].indirect(offs_t[:, cols]))
+            gs = keep.tile([P, GCUT], U8, name="g_scales%d" % c, align_bytes=64)
+            nc.vector.tensor_copy(gs[:], x_scales[:].indirect(offs_t[:, cols]))
+            g_codes.append(gc)
+            g_scales.append(gs)
+
+        sums = []
+        h_codes = []
+        h_scales = []
+
+        def first_layer(e):
+            c, i = divmod(e * C, GCUT)
+            if i == 0:
+                gather(c)
+            grp = keep.tile([P, PACK, P, PACK], BF16, name="w1_grp%d" % e, align_bytes=64)
+            src = w1_raw[e][:].rearrange("p j (m t) -> p m j t", t=PACK)
+            dst = grp[:].rearrange("p t m j -> p m j t")
+            if MV[e] > 0:
+                nc.vector.tensor_copy(dst[:, 0 : MV[e], :, :], src[:, 0 : MV[e], :, :])
+            if MV[e] < P:
+                nc.scalar.copy(dst[:, MV[e] : P, :, :], src[:, MV[e] : P, :, :])
+            wc = keep.tile([P, H], U32, name="w1_codes%d" % e, align_bytes=64)
+            ws = keep.tile([P, H], U8, name="w1_scales%d" % e, align_bytes=64)
+            nc.vector.quantize_mx(
+                out=wc[:].bitcast(FP8X4), scales=ws[:], in_=grp[:].rearrange("p t m j -> p (t m j)")
+            )
+            a_ps = psum_a.tile([P, PACK, C], F32, name="a_ps")
+            for t in range(PACK):
+                nc.tensor.matmul_mx(
+                    out=a_ps[:, t, :],
+                    lhsT=wc[:, t * P : (t + 1) * P].bitcast(FP8X4),
+                    lhsT_scale=ws[:, t * P : (t + 1) * P],
+                    rhs=g_codes[c][:, i : i + C].bitcast(FP8X4),
+                    rhs_scale=g_scales[c][:, i : i + C],
+                    start=True,
+                    stop=True,
+                )
+            sums.append(a_ps)
+
+        w2_codes = []
+        w2_scales = []
+        w2_of = []
+
+        def prepare_w2(q):
+            n_e = W2_CUT[q + 1] - W2_CUT[q]
+            grp = keep.tile([P, n_e, N, PACK], BF16, name="w2_grp%d" % q, tag="w2_grp%d" % q, align_bytes=64)
+            for i in range(n_e):
+                dst = grp[:, i, :, :].rearrange("p (c i) j -> p c j i", i=4)
+                src = w2_raw[q][:, i, :].rearrange("p (j c i) -> p c j i", j=PACK, i=4)
+                if q in S_W2:
+                    nc.scalar.copy(dst, src)
+                else:
+                    nc.vector.tensor_copy(dst, src)
+            wc = keep.tile([P, n_e * N], U32, name="w2_codes%d" % q, align_bytes=64)
+            ws = keep.tile([P, n_e * N], U8, name="w2_scales%d" % q, align_bytes=64)
+            nc.vector.quantize_mx(
+                out=wc[:].bitcast(FP8X4), scales=ws[:], in_=grp[:].rearrange("p e n j -> p (e n j)")
+            )
+            w2_codes.append(wc)
+            w2_scales.append(ws)
+            for i in range(n_e):
+                w2_of.append((wc[:, i * N : (i + 1) * N], ws[:, i * N : (i + 1) * N]))
+
+        def hidden(e):
+            if e in W2_BEFORE_H:
+                for q in range(len(w2_codes), W2_BEFORE_H[e] + 1):
+                    prepare_w2(q)
+            if e in H_IN_W2_RAW:
+                h_grp = keep.tile([P, C, PACK], BF16, name="h_grp%d" % e, tag="w2_raw%d" % H_IN_W2_RAW[e], align_bytes=64)
+            else:
+                h_grp = ring.tile([P, C, PACK], BF16, name="h_grp%d" % e, tag="ring", align_bytes=64)
+            nc.scalar.activation(h_grp[:], sums[e][:].rearrange("p t n -> p n t"), ACT.Gelu_apprx_tanh)
+            if e in H_AFTER_W2:
+                for q in range(len(w2_codes), H_AFTER_W2[e] + 1):
+                    prepare_w2(q)
+                hc = keep.tile([P, C], U32, name="h_codes%d" % e, tag="w2_grp%d" % H_AFTER_W2[e], align_bytes=64)
+            else:
+                hc = keep.tile([P, C], U32, name="h_codes%d" % e, align_bytes=64)
+            hs = keep.tile([P, C], U8, name="h_scales%d" % e, align_bytes=64)
+            nc.vector.quantize_mx(
+                out=hc[:].bitcast(FP8X4), scales=hs[:], in_=h_grp[:].rearrange("p n t -> p (n t)")
+            )
+            h_codes.append(hc)
+            h_scales.append(hs)
+
+        for e in range(E):
+            first_layer(e)
+            if e >= LAG:
+                hidden(e - LAG)
+        for e in range(E - LAG, E):
+            hidden(e)
+
+        y_sb = keep.tile([P, E * C], F32, name="y_sb")
+        for b in range(len(Y_CUT) - 1):
+            y_ps = psum_y.tile([P, (Y_CUT[b + 1] - Y_CUT[b]) * C], F32, name="y_ps%d" % b)
+            for e in range(Y_CUT[b], Y_CUT[b + 1]):
+                nc.tensor.matmul_mx(
+                    out=y_ps[:, (e - Y_CUT[b]) * C : (e - Y_CUT[b] + 1) * C],
+                    lhsT=w2_of[e][0].bitcast(FP8X4),
+                    lhsT_scale=w2_of[e][1],
+                    rhs=h_codes[e][:].bitcast(FP8X4),
+                    rhs_scale=h_scales[e][:],
+                    start=True,
+                    stop=True,
+                )
+            if b == len(Y_CUT) - 2:
+                nc.vector.tensor_copy(y_sb[:, Y_CUT[b] * C : Y_CUT[b + 1] * C], y_ps[:])
+            else:
+                nc.scalar.copy(y_sb[:, Y_CUT[b] * C : Y_CUT[b + 1] * C], y_ps[:])
+
+        first = keep.tile([P, T], F32, name="first")
+        nc.vector.tensor_tensor(first[:], y_sb[:].indirect(pos1_t[:]), gate_t[:, 0, :], ALU.mult)
+        second = keep.tile([P, T], F32, name="second")
+        nc.vector.tensor_tensor(second[:], y_sb[:].indirect(pos2_t[:]), gate_t[:, 1, :], ALU.mult)
+        total = keep.tile([P, T], F32, name="total")
+        nc.vector.tensor_tensor(total[:], first[:], second[:], ALU.add)
+        nc.sync.dma_start(out, total[:])

@@ -19,7 +19,7 @@ PACK = 4
 
 MV = (0, 48, 16, 80, 80, 80, 96, 128)
 XH = 256
-GCUT = 256
+G_CUT = (0, 3, 6, 8)
 H_AFTER_W2 = {7: 4}
 H_IN_W2_RAW = {5: 0, 7: 2}
 W2_BEFORE_H = {5: 0, 6: 1, 7: 2}
@@ -91,10 +91,11 @@ def tile_routed_moe_kernel(tc, xT, w1, w2, gate, offs, pos1, pos2, out):
         g_scales = []
 
         def gather(c):
-            cols = slice(c * GCUT // 16, (c + 1) * GCUT // 16)
-            gc = keep.tile([P, GCUT], U32, name="g_codes%d" % c, align_bytes=64)
+            cols = slice(G_CUT[c] * C // 16, G_CUT[c + 1] * C // 16)
+            n_slots = (G_CUT[c + 1] - G_CUT[c]) * C
+            gc = keep.tile([P, n_slots], U32, name="g_codes%d" % c, align_bytes=64)
             nc.vector.tensor_copy(gc[:], x_codes[:].indirect(offs_t[:, cols]))
-            gs = keep.tile([P, GCUT], U8, name="g_scales%d" % c, align_bytes=64)
+            gs = keep.tile([P, n_slots], U8, name="g_scales%d" % c, align_bytes=64)
             nc.vector.tensor_copy(gs[:], x_scales[:].indirect(offs_t[:, cols]))
             g_codes.append(gc)
             g_scales.append(gs)
@@ -104,7 +105,8 @@ def tile_routed_moe_kernel(tc, xT, w1, w2, gate, offs, pos1, pos2, out):
         h_scales = []
 
         def first_layer(e):
-            c, i = divmod(e * C, GCUT)
+            c = max([k for k in range(len(G_CUT) - 1) if G_CUT[k] <= e])
+            i = (e - G_CUT[c]) * C
             if i == 0:
                 gather(c)
             grp = keep.tile([P, PACK, P, PACK], BF16, name="w1_grp%d" % e, align_bytes=64)
@@ -139,13 +141,12 @@ def tile_routed_moe_kernel(tc, xT, w1, w2, gate, offs, pos1, pos2, out):
         def prepare_w2(q):
             n_e = W2_CUT[q + 1] - W2_CUT[q]
             grp = keep.tile([P, n_e, N, PACK], BF16, name="w2_grp%d" % q, tag="w2_grp%d" % q, align_bytes=64)
-            for i in range(n_e):
-                dst = grp[:, i, :, :].rearrange("p (c i) j -> p c j i", i=4)
-                src = w2_raw[q][:, i, :].rearrange("p (j c i) -> p c j i", j=PACK, i=4)
-                if q in S_W2:
-                    nc.scalar.copy(dst, src)
-                else:
-                    nc.vector.tensor_copy(dst, src)
+            dst = grp[:].rearrange("p e (c i) j -> p e c j i", i=4)
+            src = w2_raw[q][:].rearrange("p e (j c i) -> p e c j i", j=PACK, i=4)
+            if q in S_W2:
+                nc.scalar.copy(dst, src)
+            else:
+                nc.vector.tensor_copy(dst, src)
             wc = keep.tile([P, n_e * N], U32, name="w2_codes%d" % q, align_bytes=64)
             ws = keep.tile([P, n_e * N], U8, name="w2_scales%d" % q, align_bytes=64)
             nc.vector.quantize_mx(

@@ -26,6 +26,7 @@ W2_BEFORE_H = {5: 0, 6: 1, 7: 2}
 S_W2 = (0, 2)
 W2_CUT = (0, 2, 4, 6, 7, 8)
 Y_CUT = (0, 4, 6, 7, 8)
+TH = 256
 LAG = 2
 
 
@@ -204,10 +205,16 @@ def tile_routed_moe_kernel(tc, xT, w1, w2, gate, offs, pos1, pos2, out):
             else:
                 nc.scalar.copy(y_sb[:, Y_CUT[b] * C : Y_CUT[b + 1] * C], y_ps[:])
 
-        first = keep.tile([P, T], F32, name="first")
-        nc.vector.tensor_tensor(first[:], y_sb[:].indirect(pos1_t[:]), gate_t[:, 0, :], ALU.mult)
-        second = keep.tile([P, T], F32, name="second")
-        nc.vector.tensor_tensor(second[:], y_sb[:].indirect(pos2_t[:]), gate_t[:, 1, :], ALU.mult)
-        total = keep.tile([P, T], F32, name="total")
-        nc.vector.tensor_tensor(total[:], first[:], second[:], ALU.add)
-        nc.sync.dma_start(out, total[:])
+        halves = [slice(u * TH, (u + 1) * TH) for u in range(T // TH)]
+        products = []
+        for r, pos_t in enumerate((pos1_t, pos2_t)):
+            for u, cols in enumerate(halves):
+                prod = keep.tile([P, TH], F32, name="prod%d_%d" % (r, u))
+                nc.vector.tensor_tensor(
+                    prod[:], y_sb[:].indirect(pos_t[:, u * TH // 16 : (u + 1) * TH // 16]), gate_t[:, r, cols], ALU.mult
+                )
+                products.append(prod)
+        for u, cols in enumerate(halves):
+            total = keep.tile([P, TH], F32, name="total%d" % u)
+            nc.vector.tensor_tensor(total[:], products[u][:], products[T // TH + u][:], ALU.add)
+            nc.sync.dma_start(out[:, cols], total[:])

@@ -8,6 +8,7 @@ FLOPS = 2 * E * C * (K * H + H * N)
 F32 = mybir.dt.float32
 BF16 = mybir.dt.bfloat16
 U32 = mybir.dt.uint32
+I32 = mybir.dt.int32
 U16 = mybir.dt.uint16
 U8 = mybir.dt.uint8
 FP8X4 = mybir.dt.float8_e4m3fn_x4
@@ -19,7 +20,8 @@ PACK = 4
 
 MV = (0, 48, 16, 80, 80, 80, 96, 128)
 XH = 256
-G_CUT = (0, 3, 6, 8)
+G_CUT = (0, 8)
+XW = 1408
 H_AFTER_W2 = {7: 4}
 H_IN_W2_RAW = {5: 0, 7: 2}
 W2_BEFORE_H = {5: 0, 6: 1, 7: 2}
@@ -75,8 +77,10 @@ def tile_routed_moe_kernel(tc, xT, w1, w2, gate, offs, pos1, pos2, out):
         warm_out = keep.tile([P, 1], F32, name="warm_out")
         nc.vector.memset(warm_in[:], 0.0)
         nc.scalar.activation(warm_out[:], warm_in[:], ACT.Gelu_apprx_tanh)
-        x_scales = keep.tile([P, T], U8, name="x_scales", align_bytes=64)
+        x_scales = keep.tile([P, XW], U8, name="x_scales", align_bytes=64)
         nc.gpsimd.memset(x_scales[:], 0)
+        x_codes = keep.tile([P, XW], I32, name="x_codes", align_bytes=64)
+        nc.vector.memset(x_codes[:], 0)
 
         x_grp = keep.tile([P, T, PACK], BF16, name="x_grp", align_bytes=64)
         for u in range(T // XH):
@@ -84,9 +88,8 @@ def tile_routed_moe_kernel(tc, xT, w1, w2, gate, offs, pos1, pos2, out):
                 x_grp[:, u * XH : (u + 1) * XH, :].rearrange("p (c i) j -> p c j i", i=4),
                 x_raw[u][:].rearrange("p j (c i) -> p c j i", i=4),
             )
-        x_codes = keep.tile([P, T], U32, name="x_codes", align_bytes=64)
         nc.vector.quantize_mx(
-            out=x_codes[:].bitcast(FP8X4), scales=x_scales[:], in_=x_grp[:].rearrange("p t j -> p (t j)")
+            out=x_codes[:, 0:T].bitcast(FP8X4), scales=x_scales[:, 0:T], in_=x_grp[:].rearrange("p t j -> p (t j)")
         )
         g_codes = []
         g_scales = []
@@ -95,7 +98,7 @@ def tile_routed_moe_kernel(tc, xT, w1, w2, gate, offs, pos1, pos2, out):
             cols = slice(G_CUT[c] * C // 16, G_CUT[c + 1] * C // 16)
             n_slots = (G_CUT[c + 1] - G_CUT[c]) * C
             gc = keep.tile([P, n_slots], U32, name="g_codes%d" % c, align_bytes=64)
-            nc.vector.tensor_copy(gc[:], x_codes[:].indirect(offs_t[:, cols]))
+            nc.vector.tensor_copy(gc[:], x_codes[:].bitcast(U32).indirect(offs_t[:, cols]))
             gs = keep.tile([P, n_slots], U8, name="g_scales%d" % c, align_bytes=64)
             nc.vector.tensor_copy(gs[:], x_scales[:].indirect(offs_t[:, cols]))
             g_codes.append(gc)

@@ -27,7 +27,7 @@ H_IN_W2_RAW = {5: 0, 7: 2}
 W2_BEFORE_H = {5: 0, 6: 1, 7: 2}
 S_W2 = (0, 2)
 W2_CUT = (0, 2, 4, 6, 7, 8)
-Y_CUT = (0, 4, 6, 7, 8)
+Y_CUT = (0, 4, 7, 8)
 TH = 256
 LAG = 2
 
@@ -190,7 +190,7 @@ def tile_routed_moe_kernel(tc, xT, w1, w2, gate, offs, pos1, pos2, out):
         for e in range(E - LAG, E):
             hidden(e)
 
-        y_sb = keep.tile([P, E * C], F32, name="y_sb")
+        y_sb = keep.tile([P, E * C], F32, name="y_sb", tag="w2_grp2", align_bytes=64)
         for b in range(len(Y_CUT) - 1):
             y_ps = psum_y.tile([P, (Y_CUT[b + 1] - Y_CUT[b]) * C], F32, name="y_ps%d" % b)
             for e in range(Y_CUT[b], Y_CUT[b + 1]):

@@ -23,9 +23,9 @@ XH = 256
 G_CUT = (0, 8)
 XW = 1408
 H_AFTER_W2 = {7: 4}
-H_IN_W2_RAW = {5: 0, 7: 2}
+H_IN_W2_RAW = {5: "w1_grp6", 7: "w2_raw2"}
 W2_BEFORE_H = {5: 0, 6: 1, 7: 2}
-S_W2 = (0, 2)
+S_W2 = (0, 1, 4)
 W2_CUT = (0, 2, 4, 6, 7, 8)
 Y_CUT = (0, 4, 7, 8)
 TH = 256
@@ -145,12 +145,13 @@ def tile_routed_moe_kernel(tc, xT, w1, w2, gate, offs, pos1, pos2, out):
         def prepare_w2(q):
             n_e = W2_CUT[q + 1] - W2_CUT[q]
             grp = keep.tile([P, n_e, N, PACK], BF16, name="w2_grp%d" % q, tag="w2_grp%d" % q, align_bytes=64)
+            n_s = len([e for e in range(W2_CUT[q], W2_CUT[q + 1]) if e in S_W2])
             dst = grp[:].rearrange("p e (c i) j -> p e c j i", i=4)
             src = w2_raw[q][:].rearrange("p e (j c i) -> p e c j i", j=PACK, i=4)
-            if q in S_W2:
-                nc.scalar.copy(dst, src)
-            else:
-                nc.vector.tensor_copy(dst, src)
+            if n_s > 0:
+                nc.scalar.copy(dst[:, 0:n_s], src[:, 0:n_s])
+            if n_s < n_e:
+                nc.vector.tensor_copy(dst[:, n_s:n_e], src[:, n_s:n_e])
             wc = keep.tile([P, n_e * N], U32, name="w2_codes%d" % q, align_bytes=64)
             ws = keep.tile([P, n_e * N], U8, name="w2_scales%d" % q, align_bytes=64)
             nc.vector.quantize_mx(
@@ -166,7 +167,7 @@ def tile_routed_moe_kernel(tc, xT, w1, w2, gate, offs, pos1, pos2, out):
                 for q in range(len(w2_codes), W2_BEFORE_H[e] + 1):
                     prepare_w2(q)
             if e in H_IN_W2_RAW:
-                h_grp = keep.tile([P, C, PACK], BF16, name="h_grp%d" % e, tag="w2_raw%d" % H_IN_W2_RAW[e], align_bytes=64)
+                h_grp = keep.tile([P, C, PACK], BF16, name="h_grp%d" % e, tag=H_IN_W2_RAW[e], align_bytes=64)
             else:
                 h_grp = ring.tile([P, C, PACK], BF16, name="h_grp%d" % e, tag="ring", align_bytes=64)
             nc.scalar.activation(h_grp[:], sums[e][:].rearrange("p t n -> p n t"), ACT.Gelu_apprx_tanh)

@@ -19,10 +19,11 @@ P = 128
 PACK = 4
 
 MV = (0, 48, 16, 80, 80, 80, 96, 128)
-XH = 256
+XV = 320
 G_CUT = (0, 8)
 XW = 1408
 H_AFTER_W2 = {7: 4}
+H_ALIGN = {5: 64, 7: 256}
 H_IN_W2_RAW = {5: "w1_grp6", 7: "w2_raw2"}
 W2_BEFORE_H = {5: 0, 6: 1, 7: 2}
 S_W2 = (0, 1, 4)
@@ -44,33 +45,30 @@ def tile_routed_moe_kernel(tc, xT, w1, w2, gate, offs, pos1, pos2, out):
         offs_t = lists.tile([P, E * C // 16], U16, name="offs_t")
         nc.sync.dma_start(offs_t[:], offs)
         x_view = xT.rearrange("(p j) t -> p j t", j=PACK)
-        x_raw = []
-        for u in range(T // XH):
-            raw = keep.tile([P, PACK, XH], F32, name="x_raw%d" % u)
-            nc.sync.dma_start(raw[:], x_view[:, :, u * XH : (u + 1) * XH])
-            x_raw.append(raw)
+        x_raw = keep.tile([P, PACK, T], F32, name="x_raw", align_bytes=256)
+        nc.sync.dma_start(x_raw[:], x_view)
         w1_raw = []
         for e in range(E):
             if e < LAG:
-                raw = keep.tile([P, PACK, H], F32, name="w1_raw%d" % e)
+                raw = keep.tile([P, PACK, H], F32, name="w1_raw%d" % e, align_bytes=256)
             else:
-                raw = ring.tile([P, PACK, H], F32, name="w1_raw%d" % e, tag="ring", align_bytes=64)
+                raw = ring.tile([P, PACK, H], F32, name="w1_raw%d" % e, tag="ring", align_bytes=256)
             nc.sync.dma_start(raw[:], w1[e, :, :].rearrange("(p j) c -> p j c", j=PACK))
             w1_raw.append(raw)
-        pos1_t = lists.tile([P, T // 16], U16, name="pos1_t")
-        nc.sync.dma_start(pos1_t[:], pos1)
-        pos2_t = lists.tile([P, T // 16], U16, name="pos2_t")
-        nc.sync.dma_start(pos2_t[:], pos2)
         w2_raw = []
         for q in range(len(W2_CUT) - 1):
             raw = keep.tile(
-                [P, W2_CUT[q + 1] - W2_CUT[q], PACK * N], F32, name="w2_raw%d" % q, tag="w2_raw%d" % q, align_bytes=64
+                [P, W2_CUT[q + 1] - W2_CUT[q], PACK * N], F32, name="w2_raw%d" % q, tag="w2_raw%d" % q, align_bytes=256
             )
             nc.sync.dma_start(
                 raw[:], w2[W2_CUT[q] : W2_CUT[q + 1], :, :].rearrange("e (p j) n -> p e (j n)", j=PACK)
             )
             w2_raw.append(raw)
-        gate_t = keep.tile([P, 2, T], F32, name="gate_t")
+        pos1_t = lists.tile([P, T // 16], U16, name="pos1_t")
+        nc.sync.dma_start(pos1_t[:], pos1)
+        pos2_t = lists.tile([P, T // 16], U16, name="pos2_t")
+        nc.sync.dma_start(pos2_t[:], pos2)
+        gate_t = keep.tile([P, 2, T], F32, name="gate_t", align_bytes=256)
         nc.sync.dma_start(gate_t[:], gate.rearrange("r n t -> n r t"))
 
         warm_in = keep.tile([P, 1], F32, name="warm_in")
@@ -83,11 +81,10 @@ def tile_routed_moe_kernel(tc, xT, w1, w2, gate, offs, pos1, pos2, out):
         nc.vector.memset(x_codes[:], 0)
 
         x_grp = keep.tile([P, T, PACK], BF16, name="x_grp", align_bytes=64)
-        for u in range(T // XH):
-            nc.vector.tensor_copy(
-                x_grp[:, u * XH : (u + 1) * XH, :].rearrange("p (c i) j -> p c j i", i=4),
-                x_raw[u][:].rearrange("p j (c i) -> p c j i", i=4),
-            )
+        x_dst = x_grp[:].rearrange("p (c i) j -> p c j i", i=4)
+        x_src = x_raw[:].rearrange("p j (c i) -> p c j i", i=4)
+        nc.vector.tensor_copy(x_dst[:, 0 : XV // 4], x_src[:, 0 : XV // 4])
+        nc.scalar.copy(x_dst[:, XV // 4 : T // 4], x_src[:, XV // 4 : T // 4])
         nc.vector.quantize_mx(
             out=x_codes[:, 0:T].bitcast(FP8X4), scales=x_scales[:, 0:T], in_=x_grp[:].rearrange("p t j -> p (t j)")
         )
@@ -167,9 +164,9 @@ def tile_routed_moe_kernel(tc, xT, w1, w2, gate, offs, pos1, pos2, out):
                 for q in range(len(w2_codes), W2_BEFORE_H[e] + 1):
                     prepare_w2(q)
             if e in H_IN_W2_RAW:
-                h_grp = keep.tile([P, C, PACK], BF16, name="h_grp%d" % e, tag=H_IN_W2_RAW[e], align_bytes=64)
+                h_grp = keep.tile([P, C, PACK], BF16, name="h_grp%d" % e, tag=H_IN_W2_RAW[e], align_bytes=H_ALIGN[e])
             else:
-                h_grp = ring.tile([P, C, PACK], BF16, name="h_grp%d" % e, tag="ring", align_bytes=64)
+                h_grp = ring.tile([P, C, PACK], BF16, name="h_grp%d" % e, tag="ring", align_bytes=256)
             nc.scalar.activation(h_grp[:], sums[e][:].rearrange("p t n -> p n t"), ACT.Gelu_apprx_tanh)
             if e in H_AFTER_W2:
                 for q in range(len(w2_codes), H_AFTER_W2[e] + 1):

@@ -22,7 +22,7 @@ MV = (0, 48, 16, 80, 80, 80, 96, 128)
 XV = 320
 G_CUT = (0, 8)
 XW = 1408
-H_AFTER_W2 = {7: 4}
+H_AFTER_W2 = {7: 3}
 H_ALIGN = {5: 64, 7: 256}
 H_IN_W2_RAW = {5: "w1_grp6", 7: "w2_raw2"}
 W2_BEFORE_H = {5: 0, 6: 1, 7: 2}
@@ -188,6 +188,9 @@ def tile_routed_moe_kernel(tc, xT, w1, w2, gate, offs, pos1, pos2, out):
         for e in range(E - LAG, E):
             hidden(e)
 
+        for q in range(len(w2_codes), len(W2_CUT) - 1):
+            prepare_w2(q)
+
         y_sb = keep.tile([P, E * C], F32, name="y_sb", tag="w2_grp2", align_bytes=64)
         for b in range(len(Y_CUT) - 1):
             y_ps = psum_y.tile([P, (Y_CUT[b + 1] - Y_CUT[b]) * C], F32, name="y_ps%d" % b)
@@ -207,15 +210,16 @@ def tile_routed_moe_kernel(tc, xT, w1, w2, gate, offs, pos1, pos2, out):
                 nc.scalar.copy(y_sb[:, Y_CUT[b] * C : Y_CUT[b + 1] * C], y_ps[:])
 
         halves = [slice(u * TH, (u + 1) * TH) for u in range(T // TH)]
-        products = []
-        for r, pos_t in enumerate((pos1_t, pos2_t)):
-            for u, cols in enumerate(halves):
-                prod = keep.tile([P, TH], F32, name="prod%d_%d" % (r, u))
-                nc.vector.tensor_tensor(
-                    prod[:], y_sb[:].indirect(pos_t[:, u * TH // 16 : (u + 1) * TH // 16]), gate_t[:, r, cols], ALU.mult
-                )
-                products.append(prod)
+        first = keep.tile([P, T], F32, name="first")
+        nc.vector.tensor_tensor(first[:], y_sb[:].indirect(pos1_t[:]), gate_t[:, 0, :], ALU.mult)
+        second = []
+        for u, cols in enumerate(halves):
+            prod = keep.tile([P, TH], F32, name="second%d" % u)
+            nc.vector.tensor_tensor(
+                prod[:], y_sb[:].indirect(pos2_t[:, u * TH // 16 : (u + 1) * TH // 16]), gate_t[:, 1, cols], ALU.mult
+            )
+            second.append(prod)
         for u, cols in enumerate(halves):
             total = keep.tile([P, TH], F32, name="total%d" % u)
-            nc.vector.tensor_tensor(total[:], products[u][:], products[T // TH + u][:], ALU.add)
+            nc.vector.tensor_tensor(total[:], first[:, cols], second[u][:], ALU.add)
             nc.sync.dma_start(out[:, cols], total[:])

from contextlib import ExitStack

import concourse.mybir as mybir

K, T, E, C, H, N = 512, 512, 8, 128, 512, 128
FLOPS = 2 * E * C * (K * H + H * N)

F32 = mybir.dt.float32
BF16 = mybir.dt.bfloat16
U32 = mybir.dt.uint32
I32 = mybir.dt.int32
U16 = mybir.dt.uint16
U8 = mybir.dt.uint8
FP8X4 = mybir.dt.float8_e4m3fn_x4
ACT = mybir.ActivationFunctionType
ALU = mybir.AluOpType

P = 128
PACK = 4

MV = (0, 48, 16, 80, 80, 80, 96, 128)
XV = 320
G_CUT = (0, 8)
XW = 1408
H_AFTER_W2 = {7: 3}
H_ALIGN = {5: 64, 7: 256}
H_IN_W2_RAW = {5: "w1_grp6", 7: "w2_raw2"}
W2_BEFORE_H = {5: 0, 6: 1, 7: 2}
S_W2 = (0, 1, 4)
W2_CUT = (0, 2, 4, 6, 7, 8)
Y_CUT = (0, 4, 7, 8)
TH = 256
LAG = 2


def tile_routed_moe_kernel(tc, xT, w1, w2, gate, offs, pos1, pos2, out):
    nc = tc.nc
    with ExitStack() as ctx:
        lists = ctx.enter_context(tc.tile_pool(name="lists", bufs=1))
        keep = ctx.enter_context(tc.tile_pool(name="keep", bufs=1))
        ring = ctx.enter_context(tc.tile_pool(name="ring", bufs=E - LAG))
        psum_a = ctx.enter_context(tc.psum_pool(name="psum_a", bufs=4))
        psum_y = ctx.enter_context(tc.psum_pool(name="psum_y", bufs=1))

        offs_t = lists.tile([P, E * C // 16], U16, name="offs_t")
        nc.sync.dma_start(offs_t[:], offs)
        x_view = xT.rearrange("(p j) t -> p j t", j=PACK)
        x_raw = keep.tile([P, PACK, T], F32, name="x_raw", align_bytes=256)
        nc.sync.dma_start(x_raw[:], x_view)
        w1_raw = []
        for e in range(E):
            if e < LAG:
                raw = keep.tile([P, PACK, H], F32, name="w1_raw%d" % e, align_bytes=256)
            else:
                raw = ring.tile([P, PACK, H], F32, name="w1_raw%d" % e, tag="ring", align_bytes=256)
            nc.sync.dma_start(raw[:], w1[e, :, :].rearrange("(p j) c -> p j c", j=PACK))
            w1_raw.append(raw)
        w2_raw = []
        for q in range(len(W2_CUT) - 1):
            raw = keep.tile(
                [P, W2_CUT[q + 1] - W2_CUT[q], PACK * N], F32, name="w2_raw%d" % q, tag="w2_raw%d" % q, align_bytes=256
            )
            nc.sync.dma_start(
                raw[:], w2[W2_CUT[q] : W2_CUT[q + 1], :, :].rearrange("e (p j) n -> p e (j n)", j=PACK)
            )
            w2_raw.append(raw)
        pos1_t = lists.tile([P, T // 16], U16, name="pos1_t")
        nc.sync.dma_start(pos1_t[:], pos1)
        pos2_t = lists.tile([P, T // 16], U16, name="pos2_t")
        nc.sync.dma_start(pos2_t[:], pos2)
        gate_t = keep.tile([P, 2, T], F32, name="gate_t", align_bytes=256)
        nc.sync.dma_start(gate_t[:], gate.rearrange("r n t -> n r t"))

        warm_in = keep.tile([P, 1], F32, name="warm_in")
        warm_out = keep.tile([P, 1], F32, name="warm_out")
        nc.vector.memset(warm_in[:], 0.0)
        nc.scalar.activation(warm_out[:], warm_in[:], ACT.Gelu_apprx_tanh)
        x_scales = keep.tile([P, XW], U8, name="x_scales", align_bytes=64)
        nc.gpsimd.memset(x_scales[:], 0)
        x_codes = keep.tile([P, XW], I32, name="x_codes", align_bytes=64)
        nc.vector.memset(x_codes[:], 0)

        x_grp = keep.tile([P, T, PACK], BF16, name="x_grp", align_bytes=64)
        x_dst = x_grp[:].rearrange("p (c i) j -> p c j i", i=4)
        x_src = x_raw[:].rearrange("p j (c i) -> p c j i", i=4)
        nc.vector.tensor_copy(x_dst[:, 0 : XV // 4], x_src[:, 0 : XV // 4])
        nc.scalar.copy(x_dst[:, XV // 4 : T // 4], x_src[:, XV // 4 : T // 4])
        nc.vector.quantize_mx(
            out=x_codes[:, 0:T].bitcast(FP8X4), scales=x_scales[:, 0:T], in_=x_grp[:].rearrange("p t j -> p (t j)")
        )
        g_codes = []
        g_scales = []

        def gather(c):
            cols = slice(G_CUT[c] * C // 16, G_CUT[c + 1] * C // 16)
            n_slots = (G_CUT[c + 1] - G_CUT[c]) * C
            gc = keep.tile([P, n_slots], U32, name="g_codes%d" % c, align_bytes=64)
            nc.vector.tensor_copy(gc[:], x_codes[:].bitcast(U32).indirect(offs_t[:, cols]))
            gs = keep.tile([P, n_slots], U8, name="g_scales%d" % c, align_bytes=64)
            nc.vector.tensor_copy(gs[:], x_scales[:].indirect(offs_t[:, cols]))
            g_codes.append(gc)
            g_scales.append(gs)

        sums = []
        h_codes = []
        h_scales = []

        def first_layer(e):
            c = max([k for k in range(len(G_CUT) - 1) if G_CUT[k] <= e])
            i = (e - G_CUT[c]) * C
            if i == 0:
                gather(c)
            grp = keep.tile([P, PACK, P, PACK], BF16, name="w1_grp%d" % e, align_bytes=64)
            src = w1_raw[e][:].rearrange("p j (m t) -> p m j t", t=PACK)
            dst = grp[:].rearrange("p t m j -> p m j t")
            if MV[e] > 0:
                nc.vector.tensor_copy(dst[:, 0 : MV[e], :, :], src[:, 0 : MV[e], :, :])
            if MV[e] < P:
                nc.scalar.copy(dst[:, MV[e] : P, :, :], src[:, MV[e] : P, :, :])
            wc = keep.tile([P, H], U32, name="w1_codes%d" % e, align_bytes=64)
            ws = keep.tile([P, H], U8, name="w1_scales%d" % e, align_bytes=64)
            nc.vector.quantize_mx(
                out=wc[:].bitcast(FP8X4), scales=ws[:], in_=grp[:].rearrange("p t m j -> p (t m j)")
            )
            a_ps = psum_a.tile([P, PACK, C], F32, name="a_ps")
            for t in range(PACK):
                nc.tensor.matmul_mx(
                    out=a_ps[:, t, :],
                    lhsT=wc[:, t * P : (t + 1) * P].bitcast(FP8X4),
                    lhsT_scale=ws[:, t * P : (t + 1) * P],
                    rhs=g_codes[c][:, i : i + C].bitcast(FP8X4),
                    rhs_scale=g_scales[c][:, i : i + C],
                    start=True,
                    stop=True,
                )
            sums.append(a_ps)

        w2_codes = []
        w2_scales = []
        w2_of = []

        def prepare_w2(q):
            n_e = W2_CUT[q + 1] - W2_CUT[q]
            grp = keep.tile([P, n_e, N, PACK], BF16, name="w2_grp%d" % q, tag="w2_grp%d" % q, align_bytes=64)
            n_s = len([e for e in range(W2_CUT[q], W2_CUT[q + 1]) if e in S_W2])
            dst = grp[:].rearrange("p e (c i) j -> p e c j i", i=4)
            src = w2_raw[q][:].rearrange("p e (j c i) -> p e c j i", j=PACK, i=4)
            if n_s > 0:
                nc.scalar.copy(dst[:, 0:n_s], src[:, 0:n_s])
            if n_s < n_e:
                nc.vector.tensor_copy(dst[:, n_s:n_e], src[:, n_s:n_e])
            wc = keep.tile([P, n_e * N], U32, name="w2_codes%d" % q, align_bytes=64)
            ws = keep.tile([P, n_e * N], U8, name="w2_scales%d" % q, align_bytes=64)
            nc.vector.quantize_mx(
                out=wc[:].bitcast(FP8X4), scales=ws[:], in_=grp[:].rearrange("p e n j -> p (e n j)")
            )
            w2_codes.append(wc)
            w2_scales.append(ws)
            for i in range(n_e):
                w2_of.append((wc[:, i * N : (i + 1) * N], ws[:, i * N : (i + 1) * N]))

        def hidden(e):
            if e in W2_BEFORE_H:
                for q in range(len(w2_codes), W2_BEFORE_H[e] + 1):
                    prepare_w2(q)
            if e in H_IN_W2_RAW:
                h_grp = keep.tile([P, C, PACK], BF16, name="h_grp%d" % e, tag=H_IN_W2_RAW[e], align_bytes=H_ALIGN[e])
            else:
                h_grp = ring.tile([P, C, PACK], BF16, name="h_grp%d" % e, tag="ring", align_bytes=256)
            nc.scalar.activation(h_grp[:], sums[e][:].rearrange("p t n -> p n t"), ACT.Gelu_apprx_tanh)
            if e in H_AFTER_W2:
                for q in range(len(w2_codes), H_AFTER_W2[e] + 1):
                    prepare_w2(q)
                hc = keep.tile([P, C], U32, name="h_codes%d" % e, tag="w2_grp%d" % H_AFTER_W2[e], align_bytes=64)
            else:
                hc = keep.tile([P, C], U32, name="h_codes%d" % e, align_bytes=64)
            hs = keep.tile([P, C], U8, name="h_scales%d" % e, align_bytes=64)
            nc.vector.quantize_mx(
                out=hc[:].bitcast(FP8X4), scales=hs[:], in_=h_grp[:].rearrange("p n t -> p (n t)")
            )
            h_codes.append(hc)
            h_scales.append(hs)

        for e in range(E):
            first_layer(e)
            if e >= LAG:
                hidden(e - LAG)
        for e in range(E - LAG, E):
            hidden(e)

        for q in range(len(w2_codes), len(W2_CUT) - 1):
            prepare_w2(q)

        y_sb = keep.tile([P, E * C], F32, name="y_sb", tag="w2_grp2", align_bytes=64)
        for b in range(len(Y_CUT) - 1):
            y_ps = psum_y.tile([P, (Y_CUT[b + 1] - Y_CUT[b]) * C], F32, name="y_ps%d" % b)
            for e in range(Y_CUT[b], Y_CUT[b + 1]):
                nc.tensor.matmul_mx(
                    out=y_ps[:, (e - Y_CUT[b]) * C : (e - Y_CUT[b] + 1) * C],
                    lhsT=w2_of[e][0].bitcast(FP8X4),
                    lhsT_scale=w2_of[e][1],
                    rhs=h_codes[e][:].bitcast(FP8X4),
                    rhs_scale=h_scales[e][:],
                    start=True,
                    stop=True,
                )
            if b == len(Y_CUT) - 2:
                nc.vector.tensor_copy(y_sb[:, Y_CUT[b] * C : Y_CUT[b + 1] * C], y_ps[:])
            else:
                nc.scalar.copy(y_sb[:, Y_CUT[b] * C : Y_CUT[b + 1] * C], y_ps[:])

        halves = [slice(u * TH, (u + 1) * TH) for u in range(T // TH)]
        first = keep.tile([P, T], F32, name="first")
        nc.vector.tensor_tensor(first[:], y_sb[:].indirect(pos1_t[:]), gate_t[:, 0, :], ALU.mult)
        second = []
        for u, cols in enumerate(halves):
            prod = keep.tile([P, TH], F32, name="second%d" % u)
            nc.vector.tensor_tensor(
                prod[:], y_sb[:].indirect(pos2_t[:, u * TH // 16 : (u + 1) * TH // 16]), gate_t[:, 1, cols], ALU.mult
            )
            second.append(prod)
        for u, cols in enumerate(halves):
            total = keep.tile([P, TH], F32, name="total%d" % u)
            nc.vector.tensor_tensor(total[:], first[:, cols], second[u][:], ALU.add)
            nc.sync.dma_start(out[:, cols], total[:])
